import numpy as np
import ml_dtypes


def mxq(x, axis, fmt="e4m3"):
    dtype, down = {"e4m3": (ml_dtypes.float8_e4m3fn, 7), "e5m2": (ml_dtypes.float8_e5m2, 14)}[fmt]
    v = np.moveaxis(np.asarray(x, np.float32).astype(ml_dtypes.bfloat16).astype(np.float64), axis, -1)
    blocks = v.reshape(v.shape[:-1] + (-1, 32))
    amax = np.abs(blocks).max(-1, keepdims=True)
    byte = np.maximum(np.where(amax > 0, np.frexp(amax)[1] - 1 + 127, 0) - down, 1)
    scale = np.exp2(byte - 127.0)
    codes = (blocks / scale).astype(np.float32).astype(dtype).astype(np.float64)
    return np.moveaxis((codes * scale).reshape(v.shape), -1, axis)


WIDE = False


def mx_kscale(k):
    if not WIDE:
        return np.ones(k)
    levels = np.array([10, -10, 5, -5, 0])
    if k % 512:
        return np.exp2(np.random.permutation(np.resize(levels, k // 32))).repeat(32)
    a = np.empty((k // 512, 16))
    for p in range(k // 512):
        a[p, :8] = np.random.permutation(np.resize(levels, 8))
        for g in range(8):
            far = levels[np.abs(levels - a[p, g]) >= 10]
            a[p, g + 8] = far[np.random.randint(len(far))]
    return np.exp2(a.ravel()).repeat(32)


def f64(x):
    return np.asarray(x).astype(np.float64)


def striped(idx):
    return np.tile(idx.reshape(-1, 16).T, (8, 1)).astype(np.uint16)


def unstriped(offs):
    return offs[:16].T.reshape(-1).astype(np.int64)


def relu(v):
    return np.maximum(v, 0.0)


K, T, E, C, H, N = 2048, 512, 4, 256, 512, 128


def by_expert(wq, xq):
    return np.concatenate([wq[e].T @ xq[:, e * C:(e + 1) * C] for e in range(E)], axis=1)


def setup_inputs():
    n = np.random.standard_normal
    s = mx_kscale(K)[:, None]
    u = mx_kscale(H)
    first = np.random.permutation(np.repeat(np.arange(E), T // E))
    second = (first + 1 + np.random.permutation(np.repeat(np.arange(E - 1), -(-T // (E - 1)))[:T])) % E
    while np.bincount(second, minlength=E).max() != T // E:
        load = np.bincount(second, minlength=E); hi, lo = int(load.argmax()), int(load.argmin())
        t = np.flatnonzero((second == hi) & (first != lo))[0]; second[t] = lo
    slot_token = np.empty(E * C, np.int64); pos = np.empty((2, T), np.int64); fill = np.zeros(E, np.int64)
    place = np.stack([np.random.permutation(C) for _ in range(E)])
    for r, deal in enumerate((first, second)):
        for t in np.random.permutation(T):
            e = deal[t]; j = e * C + place[e, fill[e]]; fill[e] += 1; slot_token[j] = t; pos[r, t] = j
    g = np.random.uniform(0.2, 0.8, T)
    return {
        "xT": (n((K, T)) * s).astype(np.float32),
        "w1": (n((E, K, H)) / np.sqrt(K) / s[None] * u[None, None, :]).astype(np.float32),
        "w2": (n((E, H, N)) / np.sqrt(H) / u[None, :, None]).astype(np.float32),
        "gate": np.stack([np.tile(g, (N, 1)), np.tile(1.0 - g, (N, 1))]).astype(np.float32),
        "offs": striped(slot_token),
        "pos1": striped(pos[0]),
        "pos2": striped(pos[1]),
    }


def reference(xT, w1, w2, gate, offs, pos1, pos2):
    idx = unstriped(offs)
    xq = mxq(f64(xT)[:, idx], 0, "e4m3")
    h = relu(by_expert(mxq(f64(w1), 1, "e4m3"), xq))
    y = by_expert(mxq(f64(w2), 1, "e4m3"), mxq(h, 0, "e4m3"))
    return f64(gate[0]) * y[:, unstriped(pos1)] + f64(gate[1]) * y[:, unstriped(pos2)]

@@ -1,0 +1,232 @@
+from contextlib import ExitStack
+
+import concourse.mybir as mybir
+
+K, T, E, C, H, N = 2048, 512, 4, 256, 512, 128
+FLOPS = 2 * E * C * (K * H + H * N)
+
+F32 = mybir.dt.float32
+BF16 = mybir.dt.bfloat16
+U32 = mybir.dt.uint32
+U16 = mybir.dt.uint16
+U8 = mybir.dt.uint8
+FP8X4 = mybir.dt.float8_e4m3fn_x4
+RELU = mybir.ActivationFunctionType.Relu
+MULT = mybir.AluOpType.mult
+ADD = mybir.AluOpType.add
+MAX = mybir.AluOpType.max
+
+P = 128
+PACK = 4
+K_PASS = P * PACK
+PASSES = K // K_PASS
+
+RAW_BUFS = 12
+GRP_BUFS = 6
+WQ_BUFS = 4
+X_VECTOR_TOKENS = [256,0,0,0]
+W_VECTOR_M = [0,0,0,0,0,128,0,128,0,128,0,128,48,48,48,0]
+RUN = 8
+GROUPS = [(0, 2), (2, 2), (4, 2), (6, 2), (8, 2), (10, 2), (12, 1), (13, 1), (14, 1), (15, 1)]
+GROUP_OF = dict((k, (first, width)) for first, width in GROUPS for k in range(first, first + width))
+LAST_VECTOR_M = 40
+CUTS = [(0, 384), (384, 768), (768, 1024)]
+CUT_AFTER_CHUNK = [-1,-1,-1]
+
+
+def tile_routed_moe_kernel(tc, xT, w1, w2, gate, offs, pos1, pos2, out):
+    nc = tc.nc
+    with ExitStack() as ctx:
+        lists = ctx.enter_context(tc.tile_pool(name="lists", bufs=1))
+        keep = ctx.enter_context(tc.tile_pool(name="keep", bufs=1))
+        raws = ctx.enter_context(tc.tile_pool(name="raws", bufs=RAW_BUFS))
+        grps = ctx.enter_context(tc.tile_pool(name="grps", bufs=GRP_BUFS))
+        wq = ctx.enter_context(tc.tile_pool(name="wq", bufs=WQ_BUFS))
+        hp = ctx.enter_context(tc.tile_pool(name="hp", bufs=2))
+        accs = ctx.enter_context(tc.psum_pool(name="accs", bufs=1))
+        yps = ctx.enter_context(tc.psum_pool(name="yps", bufs=3))
+
+        offs_t = lists.tile([P, E * C // 16], U16, name="offs_t")
+        pos1_t = lists.tile([P, T // 16], U16, name="pos1_t")
+        pos2_t = lists.tile([P, T // 16], U16, name="pos2_t")
+
+        x_words = [keep.tile([P, T], U32, name="x_words%d" % g, align_bytes=64) for g in range(PASSES)]
+        x_bytes = keep.tile([P, T], U8, name="x_bytes", align_bytes=64)
+        nc.gpsimd.memset(x_bytes[:], 0)
+        slot_words = keep.tile([P, PASSES, E * C], U32, name="slot_words", align_bytes=64)
+        slot_bytes = keep.tile([P, E * C], U8, name="slot_bytes", align_bytes=64)
+        h_words = [keep.tile([P, C], U32, name="h_words%d" % e, align_bytes=64) for e in range(E)]
+        h_bytes = [keep.tile([P, C], U8, name="h_bytes%d" % e, align_bytes=64) for e in range(E)]
+        w2_raw = keep.tile([P, E, PACK, N], F32, name="w2_raw")
+        w2_grp = keep.tile([P, E * N * PACK], BF16, name="w2_grp", align_bytes=64)
+        w2_words = keep.tile([P, E * N], U32, name="w2_words", align_bytes=64)
+        w2_bytes = keep.tile([P, E * N], U8, name="w2_bytes", align_bytes=64)
+        gate_t = keep.tile([P, 2, T], F32, name="gate_t")
+        y_all = keep.tile([P, E * C], F32, name="y_all")
+        part1 = keep.tile([P, T], F32, name="part1")
+        part2 = keep.tile([P, T], F32, name="part2")
+        total = keep.tile([P, T], F32, name="total")
+
+        chunks = [("x", 0, g) for g in range(PASSES)] + [("w", e, g) for e in range(E) for g in range(PASSES)]
+        last = len(chunks) - 1
+        raw_of = {}
+
+        def load(n):
+            kind, e, g = chunks[n]
+            raw = raws.tile([P, PACK, 512], F32, name="raw")
+            rows = slice(g * K_PASS, (g + 1) * K_PASS)
+            src = (xT[rows, :] if kind == "x" else w1[e, rows, :]).rearrange("(p j) c -> p j c", j=PACK)
+            if n == 0 or n == last:
+                nc.sync.dma_start(out=raw[:, :, 0:256], in_=src[:, :, 0:256])
+                nc.sync.dma_start(out=raw[:, :, 256:512], in_=src[:, :, 256:512])
+                if n == 0:
+                    nc.sync.dma_start(offs_t[:], offs)
+            else:
+                nc.sync.dma_start(out=raw[:], in_=src)
+            raw_of[n] = raw
+
+        def gather_words(cut, g):
+            lo, hi = CUTS[cut]
+            nc.vector.tensor_copy(slot_words[:, g, lo:hi], x_words[g][:].indirect(offs_t[:, lo // 16 : hi // 16]))
+
+        def gather_bytes(cut):
+            lo, hi = CUTS[cut]
+            nc.vector.tensor_copy(slot_bytes[:, lo:hi], x_bytes[:].indirect(offs_t[:, lo // 16 : hi // 16]))
+
+        ahead = RAW_BUFS - 2
+        for n in range(ahead):
+            load(n)
+
+        acc = {}
+        for n in range(len(chunks)):
+            if n + ahead < len(chunks):
+                load(n + ahead)
+            if n + ahead == len(chunks):
+                w2_view = w2.rearrange("e (p t) n -> p e (t n)", t=PACK)
+                nc.sync.dma_start(out=w2_raw[:, 0:2, :, :].rearrange("p e t n -> p e (t n)"), in_=w2_view[:, 0:2, :])
+                nc.sync.dma_start(out=w2_raw[:, 2:4, :, :].rearrange("p e t n -> p e (t n)"), in_=w2_view[:, 2:4, :])
+                nc.sync.dma_start(out=gate_t[:], in_=gate.rearrange("a n t -> n a t"))
+                nc.sync.dma_start(pos1_t[:], pos1)
+                nc.sync.dma_start(pos2_t[:], pos2)
+            kind, e, g = chunks[n]
+            raw = raw_of[n]
+            if kind == "x":
+                grp = grps.tile([P, PACK * 512], BF16, name="grp", align_bytes=64)
+                a = X_VECTOR_TOKENS[g]
+                if a > 0:
+                    nc.vector.tensor_copy(
+                        out=grp[:, 0 : 4 * a].rearrange("p (c i j) -> p c j i", i=RUN, j=4),
+                        in_=raw[:, :, 0:a].rearrange("p j (c i) -> p c j i", i=RUN),
+                    )
+                nc.scalar.copy(
+                    out=grp[:, 4 * a : 4 * T].rearrange("p (c i j) -> p c j i", i=RUN, j=4),
+                    in_=raw[:, :, a:T].rearrange("p j (c i) -> p c j i", i=RUN),
+                )
+                nc.vector.quantize_mx(out=x_words[g][:].bitcast(FP8X4), scales=x_bytes[4 * g : P, :], in_=grp[:])
+                for cut in range(len(CUTS)):
+                    if CUT_AFTER_CHUNK[cut] < 0:
+                        gather_words(cut, g)
+                        if g == PASSES - 1:
+                            gather_bytes(cut)
+                continue
+
+            k = n - PASSES
+            first, width = GROUP_OF[k]
+            if k == first:
+                grp = grps.tile([P, width * PACK * H], BF16, name="grp", align_bytes=64)
+                w_words = wq.tile([P, width * H], U32, name="w_words", align_bytes=64)
+                w_bytes = wq.tile([P, width * H], U8, name="w_bytes", align_bytes=64)
+            part = grp[:, (k - first) * PACK * H : (k - first + 1) * PACK * H]
+            dst = part.rearrange("p (t a b j) -> p a j b t", t=4, b=2, j=4)
+            src = raw[:].rearrange("p j (a b t) -> p a j b t", b=2, t=4)
+            if n == last:
+                for m0 in (0, 64):
+                    m1 = m0 + LAST_VECTOR_M
+                    nc.vector.tensor_copy(out=dst[:, m0 // 2 : m1 // 2, :, :, :], in_=src[:, m0 // 2 : m1 // 2, :, :, :])
+                    nc.scalar.copy(out=dst[:, m1 // 2 : m0 // 2 + 32, :, :, :], in_=src[:, m1 // 2 : m0 // 2 + 32, :, :, :])
+            else:
+                a = W_VECTOR_M[k]
+                if a > 0:
+                    nc.vector.tensor_copy(out=dst[:, 0 : a // 2, :, :, :], in_=src[:, 0 : a // 2, :, :, :])
+                if a < P:
+                    nc.scalar.copy(out=dst[:, a // 2 : P // 2, :, :, :], in_=src[:, a // 2 : P // 2, :, :, :])
+            if k < first + width - 1:
+                continue
+            pieces = 2 if n == last else 1
+            step = width * H // pieces
+            for q in range(pieces):
+                nc.vector.quantize_mx(
+                    out=w_words[:, q * step : (q + 1) * step].bitcast(FP8X4),
+                    scales=w_bytes[:, q * step : (q + 1) * step],
+                    in_=grp[:, q * step * PACK : (q + 1) * step * PACK],
+                )
+            for kk in range(first, first + width):
+                gg = kk % PASSES
+                for t in range(PACK):
+                    if gg == 0:
+                        acc[t] = accs.tile([P, C], F32, name="acc%d" % t)
+                    cols = slice((kk - first) * H + t * P, (kk - first) * H + (t + 1) * P)
+                    nc.tensor.matmul_mx(
+                        out=acc[t][:],
+                        lhsT=w_words[:, cols].bitcast(FP8X4),
+                        lhsT_scale=w_bytes[:, cols],
+                        rhs=slot_words[:, gg, e * C : (e + 1) * C].bitcast(FP8X4),
+                        rhs_scale=slot_bytes[4 * gg : P, e * C : (e + 1) * C],
+                        start=(gg == 0),
+                        stop=(gg == PASSES - 1),
+                    )
+            if g == PASSES - 1:
+                hb = hp.tile([P, PACK, C], BF16, name="hb")
+                for t in range(PACK):
+                    if e == E - 1 and t >= 2:
+                        nc.vector.tensor_scalar_max(out=hb[:, t, :], in0=acc[t][:], scalar1=0.0)
+                    else:
+                        nc.scalar.activation(out=hb[:, t, :], in_=acc[t][:], func=RELU)
+                hg = hp.tile([P, C * PACK], BF16, name="hg", align_bytes=64)
+                nc.vector.tensor_copy(
+                    out=hg[:].rearrange("p (c i t) -> p c t i", i=RUN, t=4),
+                    in_=hb[:].rearrange("p t (c i) -> p c t i", i=RUN),
+                )
+                nc.vector.quantize_mx(out=h_words[e][:].bitcast(FP8X4), scales=h_bytes[e][:], in_=hg[:])
+            for cut in range(len(CUTS)):
+                if CUT_AFTER_CHUNK[cut] == n - PASSES:
+                    for gg in range(PASSES):
+                        gather_words(cut, gg)
+                    gather_bytes(cut)
+
+        w2_dst = w2_grp[:].rearrange("p (e c i t) -> p e c t i", e=E, i=RUN, t=4)
+        w2_src = w2_raw[:].rearrange("p e t (c i) -> p e c t i", i=RUN)
+        half_w = 2 * N
+        nc.scalar.copy(out=w2_dst[:, 0:2, :, :, :], in_=w2_src[:, 0:2, :, :, :])
+        nc.vector.quantize_mx(out=w2_words[:, 0:half_w].bitcast(FP8X4), scales=w2_bytes[:, 0:half_w], in_=w2_grp[:, 0 : PACK * half_w])
+        nc.scalar.copy(out=w2_dst[:, 2:3, :, :, :], in_=w2_src[:, 2:3, :, :, :])
+        nc.vector.tensor_copy(out=w2_dst[:, 3:4, :, :, :], in_=w2_src[:, 3:4, :, :, :])
+        nc.vector.quantize_mx(out=w2_words[:, half_w : 2 * half_w].bitcast(FP8X4), scales=w2_bytes[:, half_w : 2 * half_w], in_=w2_grp[:, PACK * half_w : 2 * PACK * half_w])
+
+        def second_layer(out_ap, e):
+            cols = slice(e * N, (e + 1) * N)
+            nc.tensor.matmul_mx(
+                out=out_ap,
+                lhsT=w2_words[:, cols].bitcast(FP8X4),
+                lhsT_scale=w2_bytes[:, cols],
+                rhs=h_words[e][:].bitcast(FP8X4),
+                rhs_scale=h_bytes[e][:],
+                start=True,
+                stop=True,
+            )
+
+        y01 = yps.tile([P, 2 * C], F32, name="y_ps")
+        second_layer(y01[:, 0:C], 0)
+        second_layer(y01[:, C : 2 * C], 1)
+        nc.scalar.copy(out=y_all[:, 0 : 2 * C], in_=y01[:])
+        y2 = yps.tile([P, 2 * C], F32, name="y_ps")
+        second_layer(y2[:, 0:C], 2)
+        nc.scalar.copy(out=y_all[:, 2 * C : 3 * C], in_=y2[:, 0:C])
+        y3 = yps.tile([P, 2 * C], F32, name="y_ps")
+        second_layer(y3[:, 0:C], 3)
+        nc.scalar.copy(out=y_all[:, 3 * C : 4 * C], in_=y3[:, 0:C])
+
+        nc.vector.tensor_tensor(out=part1[:], in0=y_all[:].indirect(pos1_t[:]), in1=gate_t[:, 0, :], op=MULT)
+        nc.vector.tensor_tensor(out=part2[:], in0=y_all[:].indirect(pos2_t[:]), in1=gate_t[:, 1, :], op=MULT)
+        nc.vector.tensor_tensor(out=total[:], in0=part1[:], in1=part2[:], op=ADD)
+        nc.sync.dma_start(out=out, in_=total[:])

@@ -76,13 +76,13 @@ def tile_routed_moe_kernel(tc, xT, w1, w2, gate, offs, pos1, pos2, out):
             raw = raws.tile([P, PACK, 512], F32, name="raw")
             rows = slice(g * K_PASS, (g + 1) * K_PASS)
             src = (xT[rows, :] if kind == "x" else w1[e, rows, :]).rearrange("(p j) c -> p j c", j=PACK)
-            if n == 0 or n == last:
+            if n == last:
                 nc.sync.dma_start(out=raw[:, :, 0:256], in_=src[:, :, 0:256])
                 nc.sync.dma_start(out=raw[:, :, 256:512], in_=src[:, :, 256:512])
-                if n == 0:
-                    nc.sync.dma_start(offs_t[:], offs)
             else:
                 nc.sync.dma_start(out=raw[:], in_=src)
+                if n == 0:
+                    nc.sync.dma_start(offs_t[:], offs)
             raw_of[n] = raw
 
         def gather_words(cut, g):

@@ -76,13 +76,9 @@ def tile_routed_moe_kernel(tc, xT, w1, w2, gate, offs, pos1, pos2, out):
             raw = raws.tile([P, PACK, 512], F32, name="raw")
             rows = slice(g * K_PASS, (g + 1) * K_PASS)
             src = (xT[rows, :] if kind == "x" else w1[e, rows, :]).rearrange("(p j) c -> p j c", j=PACK)
-            if n == last:
-                nc.sync.dma_start(out=raw[:, :, 0:256], in_=src[:, :, 0:256])
-                nc.sync.dma_start(out=raw[:, :, 256:512], in_=src[:, :, 256:512])
-            else:
-                nc.sync.dma_start(out=raw[:], in_=src)
-                if n == 0:
-                    nc.sync.dma_start(offs_t[:], offs)
+            nc.sync.dma_start(out=raw[:], in_=src)
+            if n == 0:
+                nc.sync.dma_start(offs_t[:], offs)
             raw_of[n] = raw
 
         def gather_words(cut, g):

from contextlib import ExitStack

import concourse.mybir as mybir

K, T, E, C, H, N = 2048, 512, 4, 256, 512, 128
FLOPS = 2 * E * C * (K * H + H * N)

F32 = mybir.dt.float32
BF16 = mybir.dt.bfloat16
U32 = mybir.dt.uint32
U16 = mybir.dt.uint16
U8 = mybir.dt.uint8
FP8X4 = mybir.dt.float8_e4m3fn_x4
RELU = mybir.ActivationFunctionType.Relu
MULT = mybir.AluOpType.mult
ADD = mybir.AluOpType.add
MAX = mybir.AluOpType.max

P = 128
PACK = 4
K_PASS = P * PACK
PASSES = K // K_PASS

RAW_BUFS = 12
GRP_BUFS = 6
WQ_BUFS = 4
X_VECTOR_TOKENS = [256,0,0,0]
W_VECTOR_M = [0,0,0,0,0,128,0,128,0,128,0,128,48,48,48,0]
RUN = 8
GROUPS = [(0, 2), (2, 2), (4, 2), (6, 2), (8, 2), (10, 2), (12, 1), (13, 1), (14, 1), (15, 1)]
GROUP_OF = dict((k, (first, width)) for first, width in GROUPS for k in range(first, first + width))
LAST_VECTOR_M = 40
CUTS = [(0, 384), (384, 768), (768, 1024)]
CUT_AFTER_CHUNK = [-1,-1,-1]


def tile_routed_moe_kernel(tc, xT, w1, w2, gate, offs, pos1, pos2, out):
    nc = tc.nc
    with ExitStack() as ctx:
        lists = ctx.enter_context(tc.tile_pool(name="lists", bufs=1))
        keep = ctx.enter_context(tc.tile_pool(name="keep", bufs=1))
        raws = ctx.enter_context(tc.tile_pool(name="raws", bufs=RAW_BUFS))
        grps = ctx.enter_context(tc.tile_pool(name="grps", bufs=GRP_BUFS))
        wq = ctx.enter_context(tc.tile_pool(name="wq", bufs=WQ_BUFS))
        hp = ctx.enter_context(tc.tile_pool(name="hp", bufs=2))
        accs = ctx.enter_context(tc.psum_pool(name="accs", bufs=1))
        yps = ctx.enter_context(tc.psum_pool(name="yps", bufs=3))

        offs_t = lists.tile([P, E * C // 16], U16, name="offs_t")
        pos1_t = lists.tile([P, T // 16], U16, name="pos1_t")
        pos2_t = lists.tile([P, T // 16], U16, name="pos2_t")

        x_words = [keep.tile([P, T], U32, name="x_words%d" % g, align_bytes=64) for g in range(PASSES)]
        x_bytes = keep.tile([P, T], U8, name="x_bytes", align_bytes=64)
        nc.gpsimd.memset(x_bytes[:], 0)
        slot_words = keep.tile([P, PASSES, E * C], U32, name="slot_words", align_bytes=64)
        slot_bytes = keep.tile([P, E * C], U8, name="slot_bytes", align_bytes=64)
        h_words = [keep.tile([P, C], U32, name="h_words%d" % e, align_bytes=64) for e in range(E)]
        h_bytes = [keep.tile([P, C], U8, name="h_bytes%d" % e, align_bytes=64) for e in range(E)]
        w2_raw = keep.tile([P, E, PACK, N], F32, name="w2_raw")
        w2_grp = keep.tile([P, E * N * PACK], BF16, name="w2_grp", align_bytes=64)
        w2_words = keep.tile([P, E * N], U32, name="w2_words", align_bytes=64)
        w2_bytes = keep.tile([P, E * N], U8, name="w2_bytes", align_bytes=64)
        gate_t = keep.tile([P, 2, T], F32, name="gate_t")
        y_all = keep.tile([P, E * C], F32, name="y_all")
        part1 = keep.tile([P, T], F32, name="part1")
        part2 = keep.tile([P, T], F32, name="part2")
        total = keep.tile([P, T], F32, name="total")

        chunks = [("x", 0, g) for g in range(PASSES)] + [("w", e, g) for e in range(E) for g in range(PASSES)]
        last = len(chunks) - 1
        raw_of = {}

        def load(n):
            kind, e, g = chunks[n]
            raw = raws.tile([P, PACK, 512], F32, name="raw")
            rows = slice(g * K_PASS, (g + 1) * K_PASS)
            src = (xT[rows, :] if kind == "x" else w1[e, rows, :]).rearrange("(p j) c -> p j c", j=PACK)
            nc.sync.dma_start(out=raw[:], in_=src)
            if n == 0:
                nc.sync.dma_start(offs_t[:], offs)
            raw_of[n] = raw

        def gather_words(cut, g):
            lo, hi = CUTS[cut]
            nc.vector.tensor_copy(slot_words[:, g, lo:hi], x_words[g][:].indirect(offs_t[:, lo // 16 : hi // 16]))

        def gather_bytes(cut):
            lo, hi = CUTS[cut]
            nc.vector.tensor_copy(slot_bytes[:, lo:hi], x_bytes[:].indirect(offs_t[:, lo // 16 : hi // 16]))

        ahead = RAW_BUFS - 2
        for n in range(ahead):
            load(n)

        acc = {}
        for n in range(len(chunks)):
            if n + ahead < len(chunks):
                load(n + ahead)
            if n + ahead == len(chunks):
                w2_view = w2.rearrange("e (p t) n -> p e (t n)", t=PACK)
                nc.sync.dma_start(out=w2_raw[:, 0:2, :, :].rearrange("p e t n -> p e (t n)"), in_=w2_view[:, 0:2, :])
                nc.sync.dma_start(out=w2_raw[:, 2:4, :, :].rearrange("p e t n -> p e (t n)"), in_=w2_view[:, 2:4, :])
                nc.sync.dma_start(out=gate_t[:], in_=gate.rearrange("a n t -> n a t"))
                nc.sync.dma_start(pos1_t[:], pos1)
                nc.sync.dma_start(pos2_t[:], pos2)
            kind, e, g = chunks[n]
            raw = raw_of[n]
            if kind == "x":
                grp = grps.tile([P, PACK * 512], BF16, name="grp", align_bytes=64)
                a = X_VECTOR_TOKENS[g]
                if a > 0:
                    nc.vector.tensor_copy(
                        out=grp[:, 0 : 4 * a].rearrange("p (c i j) -> p c j i", i=RUN, j=4),
                        in_=raw[:, :, 0:a].rearrange("p j (c i) -> p c j i", i=RUN),
                    )
                nc.scalar.copy(
                    out=grp[:, 4 * a : 4 * T].rearrange("p (c i j) -> p c j i", i=RUN, j=4),
                    in_=raw[:, :, a:T].rearrange("p j (c i) -> p c j i", i=RUN),
                )
                nc.vector.quantize_mx(out=x_words[g][:].bitcast(FP8X4), scales=x_bytes[4 * g : P, :], in_=grp[:])
                for cut in range(len(CUTS)):
                    if CUT_AFTER_CHUNK[cut] < 0:
                        gather_words(cut, g)
                        if g == PASSES - 1:
                            gather_bytes(cut)
                continue

            k = n - PASSES
            first, width = GROUP_OF[k]
            if k == first:
                grp = grps.tile([P, width * PACK * H], BF16, name="grp", align_bytes=64)
                w_words = wq.tile([P, width * H], U32, name="w_words", align_bytes=64)
                w_bytes = wq.tile([P, width * H], U8, name="w_bytes", align_bytes=64)
            part = grp[:, (k - first) * PACK * H : (k - first + 1) * PACK * H]
            dst = part.rearrange("p (t a b j) -> p a j b t", t=4, b=2, j=4)
            src = raw[:].rearrange("p j (a b t) -> p a j b t", b=2, t=4)
            if n == last:
                for m0 in (0, 64):
                    m1 = m0 + LAST_VECTOR_M
                    nc.vector.tensor_copy(out=dst[:, m0 // 2 : m1 // 2, :, :, :], in_=src[:, m0 // 2 : m1 // 2, :, :, :])
                    nc.scalar.copy(out=dst[:, m1 // 2 : m0 // 2 + 32, :, :, :], in_=src[:, m1 // 2 : m0 // 2 + 32, :, :, :])
            else:
                a = W_VECTOR_M[k]
                if a > 0:
                    nc.vector.tensor_copy(out=dst[:, 0 : a // 2, :, :, :], in_=src[:, 0 : a // 2, :, :, :])
                if a < P:
                    nc.scalar.copy(out=dst[:, a // 2 : P // 2, :, :, :], in_=src[:, a // 2 : P // 2, :, :, :])
            if k < first + width - 1:
                continue
            pieces = 2 if n == last else 1
            step = width * H // pieces
            for q in range(pieces):
                nc.vector.quantize_mx(
                    out=w_words[:, q * step : (q + 1) * step].bitcast(FP8X4),
                    scales=w_bytes[:, q * step : (q + 1) * step],
                    in_=grp[:, q * step * PACK : (q + 1) * step * PACK],
                )
            for kk in range(first, first + width):
                gg = kk % PASSES
                for t in range(PACK):
                    if gg == 0:
                        acc[t] = accs.tile([P, C], F32, name="acc%d" % t)
                    cols = slice((kk - first) * H + t * P, (kk - first) * H + (t + 1) * P)
                    nc.tensor.matmul_mx(
                        out=acc[t][:],
                        lhsT=w_words[:, cols].bitcast(FP8X4),
                        lhsT_scale=w_bytes[:, cols],
                        rhs=slot_words[:, gg, e * C : (e + 1) * C].bitcast(FP8X4),
                        rhs_scale=slot_bytes[4 * gg : P, e * C : (e + 1) * C],
                        start=(gg == 0),
                        stop=(gg == PASSES - 1),
                    )
            if g == PASSES - 1:
                hb = hp.tile([P, PACK, C], BF16, name="hb")
                for t in range(PACK):
                    if e == E - 1 and t >= 2:
                        nc.vector.tensor_scalar_max(out=hb[:, t, :], in0=acc[t][:], scalar1=0.0)
                    else:
                        nc.scalar.activation(out=hb[:, t, :], in_=acc[t][:], func=RELU)
                hg = hp.tile([P, C * PACK], BF16, name="hg", align_bytes=64)
                nc.vector.tensor_copy(
                    out=hg[:].rearrange("p (c i t) -> p c t i", i=RUN, t=4),
                    in_=hb[:].rearrange("p t (c i) -> p c t i", i=RUN),
                )
                nc.vector.quantize_mx(out=h_words[e][:].bitcast(FP8X4), scales=h_bytes[e][:], in_=hg[:])
            for cut in range(len(CUTS)):
                if CUT_AFTER_CHUNK[cut] == n - PASSES:
                    for gg in range(PASSES):
                        gather_words(cut, gg)
                    gather_bytes(cut)

        w2_dst = w2_grp[:].rearrange("p (e c i t) -> p e c t i", e=E, i=RUN, t=4)
        w2_src = w2_raw[:].rearrange("p e t (c i) -> p e c t i", i=RUN)
        half_w = 2 * N
        nc.scalar.copy(out=w2_dst[:, 0:2, :, :, :], in_=w2_src[:, 0:2, :, :, :])
        nc.vector.quantize_mx(out=w2_words[:, 0:half_w].bitcast(FP8X4), scales=w2_bytes[:, 0:half_w], in_=w2_grp[:, 0 : PACK * half_w])
        nc.scalar.copy(out=w2_dst[:, 2:3, :, :, :], in_=w2_src[:, 2:3, :, :, :])
        nc.vector.tensor_copy(out=w2_dst[:, 3:4, :, :, :], in_=w2_src[:, 3:4, :, :, :])
        nc.vector.quantize_mx(out=w2_words[:, half_w : 2 * half_w].bitcast(FP8X4), scales=w2_bytes[:, half_w : 2 * half_w], in_=w2_grp[:, PACK * half_w : 2 * PACK * half_w])

        def second_layer(out_ap, e):
            cols = slice(e * N, (e + 1) * N)
            nc.tensor.matmul_mx(
                out=out_ap,
                lhsT=w2_words[:, cols].bitcast(FP8X4),
                lhsT_scale=w2_bytes[:, cols],
                rhs=h_words[e][:].bitcast(FP8X4),
                rhs_scale=h_bytes[e][:],
                start=True,
                stop=True,
            )

        y01 = yps.tile([P, 2 * C], F32, name="y_ps")
        second_layer(y01[:, 0:C], 0)
        second_layer(y01[:, C : 2 * C], 1)
        nc.scalar.copy(out=y_all[:, 0 : 2 * C], in_=y01[:])
        y2 = yps.tile([P, 2 * C], F32, name="y_ps")
        second_layer(y2[:, 0:C], 2)
        nc.scalar.copy(out=y_all[:, 2 * C : 3 * C], in_=y2[:, 0:C])
        y3 = yps.tile([P, 2 * C], F32, name="y_ps")
        second_layer(y3[:, 0:C], 3)
        nc.scalar.copy(out=y_all[:, 3 * C : 4 * C], in_=y3[:, 0:C])

        nc.vector.tensor_tensor(out=part1[:], in0=y_all[:].indirect(pos1_t[:]), in1=gate_t[:, 0, :], op=MULT)
        nc.vector.tensor_tensor(out=part2[:], in0=y_all[:].indirect(pos2_t[:]), in1=gate_t[:, 1, :], op=MULT)
        nc.vector.tensor_tensor(out=total[:], in0=part1[:], in1=part2[:], op=ADD)
        nc.sync.dma_start(out=out, in_=total[:])
